import numpy as np
import ml_dtypes


def mxq(x, axis, fmt="e4m3"):
    dtype, down = {"e4m3": (ml_dtypes.float8_e4m3fn, 7), "e5m2": (ml_dtypes.float8_e5m2, 14)}[fmt]
    v = np.moveaxis(np.asarray(x, np.float32).astype(ml_dtypes.bfloat16).astype(np.float64), axis, -1)
    blocks = v.reshape(v.shape[:-1] + (-1, 32))
    amax = np.abs(blocks).max(-1, keepdims=True)
    byte = np.maximum(np.where(amax > 0, np.frexp(amax)[1] - 1 + 127, 0) - down, 1)
    scale = np.exp2(byte - 127.0)
    codes = (blocks / scale).astype(np.float32).astype(dtype).astype(np.float64)
    return np.moveaxis((codes * scale).reshape(v.shape), -1, axis)


WIDE = False


def mx_kscale(k):
    if not WIDE:
        return np.ones(k)
    levels = np.array([10, -10, 5, -5, 0])
    if k % 512:
        return np.exp2(np.random.permutation(np.resize(levels, k // 32))).repeat(32)
    a = np.empty((k // 512, 16))
    for p in range(k // 512):
        a[p, :8] = np.random.permutation(np.resize(levels, 8))
        for g in range(8):
            far = levels[np.abs(levels - a[p, g]) >= 10]
            a[p, g + 8] = far[np.random.randint(len(far))]
    return np.exp2(a.ravel()).repeat(32)


def f64(x):
    return np.asarray(x).astype(np.float64)


def striped(idx):
    return np.tile(np.asarray(idx).reshape(-1, 16).T, (8, 1)).astype(np.uint16)


def unstriped(offs):
    return offs[:16].T.reshape(-1).astype(np.int64)


E2M1 = np.array([0.0, 0.5, 1.0, 1.5, 2.0, 3.0, 4.0, 6.0, -0.0, -0.5, -1.0, -1.5, -2.0, -3.0, -4.0, -6.0])


def pack_weight(w, fmt):
    k, n = w.shape
    w = f64(np.asarray(w, np.float32).astype(ml_dtypes.bfloat16)).reshape(k // 32, 32, n)
    amax = np.abs(w).max(1)
    if fmt == "e4m3":
        byte = np.frexp(amax)[1] - 1 + 127 - 7
    else:
        mant, ex = np.frexp(amax / 6.0)
        byte = np.where(mant > 0.5, ex, ex - 1) + 127
    byte = np.clip(np.where(amax > 0, byte, 1), 1, 254)
    scaled = (w * np.exp2(127.0 - byte)[:, None, :]).reshape(k, n).astype(np.float32)
    by_word = np.ascontiguousarray(scaled.reshape(k // 512, 128, 4, n).transpose(0, 1, 3, 2))
    if fmt == "e4m3":
        words = by_word.astype(ml_dtypes.float8_e4m3fn).view(np.uint8)
    else:
        c = by_word.astype(ml_dtypes.float4_e2m1fn).view(np.uint8) & 0xF
        words = (c[..., 0::2] | (c[..., 1::2] << 4)).reshape(k // 512, 128, 2 * n)
    return np.ascontiguousarray(words), np.ascontiguousarray(byte.astype(np.uint8).reshape(k // 512, 16, n))


def unpack_weight(words, scales, fmt):
    g, _, n = scales.shape
    words = np.ascontiguousarray(words).reshape(g, 128, n, -1)
    if fmt == "e4m3":
        vals = words.view(ml_dtypes.float8_e4m3fn).astype(np.float64)
    else:
        nib = np.empty((g, 128, n, 4), np.uint8)
        nib[..., 0::2] = words & 0xF
        nib[..., 1::2] = words >> 4
        vals = E2M1[nib]
    vals = vals * np.repeat(np.exp2(scales.astype(np.float64) - 127.0), 8, axis=1)[..., None]
    return vals.transpose(0, 1, 3, 2).reshape(g * 512, n)


def sigmoid(v):
    return 1.0 / (1.0 + np.exp(-v))


D, E, T, I, Q, U = 512, 512, 1024, 256, 512, 1024


def setup_inputs():
    n = np.random.standard_normal
    idx = np.random.permutation(T)[:I]
    idx4 = np.random.permutation(U)[:I]
    fd = mx_kscale(D)
    fe = mx_kscale(E)
    fq = mx_kscale(Q)
    keysp = pack_weight(n((D, T)) / fd[:, None], "e2m1")
    valsp = pack_weight(n((E, T)) / fe[:, None], "e2m1")
    return {
        "query": (n((D, Q)) * 1.0 / np.sqrt(D) * fd[:, None]).astype(np.float32),
        "query2": (n((D, Q)) * 1.0 / np.sqrt(D) * fd[:, None]).astype(np.float32),
        "keys_words": keysp[0],
        "keys_scales": keysp[1],
        "th": (np.random.uniform(0.3, 1.5, (Q, 1))).astype(np.float32),
        "gout": (n((E, Q)) * 1 / np.sqrt(E) * fe[:, None]).astype(np.float32),
        "vals_words": valsp[0],
        "vals_scales": valsp[1],
        "size": (np.random.uniform(0.5, 2.0, (1, I))).astype(np.float32),
        "qs": (np.random.uniform(100.0, 400.0, (Q, 1)) * fq[:, None]).astype(np.float32),
        "qrows": (n((Q, D)) / fq[:, None]).astype(np.float32),
        "old": (n((D, U)) * 4.0).astype(np.float32),
        "fade": (np.random.uniform(0.5, 1.0, (1, U))).astype(np.float32),
        "offs": striped(idx),
        "offs4": striped(idx4),
    }


def reference(query, query2, keys_words, keys_scales, th, gout, vals_words, vals_scales, size, qs, qrows, old, fade, offs, offs4):
    idx = unstriped(offs)
    idx4 = unstriped(offs4)
    keysu = unpack_weight(keys_words, keys_scales, "e2m1")
    valsu = unpack_weight(vals_words, vals_scales, "e2m1")
    queryq = mxq(f64(query), 0, "e4m3")
    keysidxg = keysu[:, idx]
    a = queryq.T @ keysidxg
    query2q = mxq(f64(query2), 0, "e4m3")
    b = query2q.T @ keysidxg
    ua = sigmoid(a - f64(th))
    ub = sigmoid(b - f64(th))
    p = 1.0 - (1.0 - ua) * (1.0 - ub)
    z = np.sum(p, axis=1, keepdims=True)
    goutq = mxq(f64(gout), 0, "e4m3")
    valsidxg = valsu[:, idx]
    c0 = goutq.T @ valsidxg
    dz = np.sum(c0 * p * f64(size) / np.square(z) * (-1.0), axis=1, keepdims=True)
    dp = c0 / z * f64(size) + dz
    dua = dp * (-1.0) * (1.0 - ub) * (-1.0)
    da = dua * ua * (1.0 - ua)
    gs = da * f64(qs)
    qrowsq = mxq(f64(qrows), 0, "e4m3")
    gsq = mxq(gs, 0, "e4m3")
    gk = qrowsq.T @ gsq
    gf = np.zeros((D, U))
    gf[:, idx4] = gk
    y = f64(old) * f64(fade) + gf
    return y

@@ -1,0 +1,289 @@
+from contextlib import ExitStack
+
+import concourse.mybir as mybir
+from concourse.masks import make_identity
+
+F32 = mybir.dt.float32
+BF16 = mybir.dt.bfloat16
+I32 = mybir.dt.int32
+U32 = mybir.dt.uint32
+U16 = mybir.dt.uint16
+U8 = mybir.dt.uint8
+FP8X4 = mybir.dt.float8_e4m3fn_x4
+FP4X4 = mybir.dt.float4_e2m1fn_x4
+ALU = mybir.AluOpType
+ACT = mybir.ActivationFunctionType
+
+P = 128
+PACK = 4
+RUN = 4
+D, E, T, I, Q, U = 512, 512, 1024, 256, 512, 1024
+BANK = 512
+FLOPS = 2 * Q * I * (D + D + E + D)
+FADE_BANK = (0, 1, 2, 3, 2, 3, 4, 5)
+BACK_BANK = ((0, 1, 6, 7), (2, 3, 4, 5))
+ON_GPSIMD = ()
+ADD_ORDER = ((0, 0), (1, 0), (2, 0), (3, 0), (0, 1), (1, 1), (2, 1), (3, 1))
+TH_COL, QS_COL, SIZE_COL, FADE_COL = 0, 4, 8, 64
+
+
+def tile_attend_beitherquestion_k_kernel(tc, query, query2, keys_words, keys_scales, th, gout, vals_words, vals_scales,
+                                          size, qs, qrows, old, fade, offs, offs4, out):
+    nc = tc.nc
+    with ExitStack() as ctx:
+        sb = ctx.enter_context(tc.tile_pool(name="sb", bufs=1))
+        ps = ctx.enter_context(tc.psum_pool(name="ps", bufs=1))
+
+        def tile(shape, dtype, name):
+            return sb.tile(shape, dtype, name=name, align_bytes=64)
+
+        banks = [ps.tile([P, BANK], F32, name=f"bank{b}") for b in range(8)]
+
+        vec_rows = tile([P, P], F32, "vec_rows")
+        placed = [tile([P, U], F32, f"placed{k}") for k in range(4)]
+        for k in range(4):
+            nc.vector.memset(placed[k][:], 0.0)
+        ident = tile([P, P], F32, "ident")
+        make_identity(nc, ident[:])
+        warm_in = tile([P, 1], F32, "warm_in")
+        warm_out = tile([P, 1], F32, "warm_out")
+        nc.gpsimd.memset(warm_in[:], 0.0)
+        nc.scalar.activation(warm_out[:], warm_in[:], ACT.Sigmoid)
+
+        def load_words(src, name):
+            words = tile([P, T], U16, name)
+            nc.sync.dma_start(words[:].bitcast(I32), src[0].bitcast(I32))
+            return words
+
+        def load_bytes(src, name):
+            scale_bytes = tile([P, T], U8, name)
+            for g in range(4):
+                rows = src[0, 4 * g:4 * g + 4, :].bitcast(I32)
+                nc.sync.dma_start(scale_bytes[32 * g:32 * g + 32, :].bitcast(I32),
+                                  rows.unsqueeze(0).broadcast_to([8, 4, T // 4]))
+            return scale_bytes
+
+        def load_rows(src, name):
+            raw = tile([P, PACK, Q], F32, name)
+            nc.sync.dma_start(raw[:], src.rearrange("(p j) w -> p j w", j=PACK))
+            return raw
+
+        def load_dealt_vector(src, first):
+            nc.sync.dma_start(vec_rows[first:first + PACK, :].rearrange("r (c i) -> r c i", i=RUN),
+                              src.rearrange("(c r i) o -> r c (i o)", r=PACK, i=RUN))
+
+        slots = sb.tile([P, I // 16], U16, name="slots")
+        places = sb.tile([P, I // 16], U16, name="places")
+        nc.sync.dma_start(slots[:], offs)
+        key_words = load_words(keys_words, "key_words")
+        key_bytes = load_bytes(keys_scales, "key_bytes")
+        qa_raw = load_rows(query, "qa_raw")
+        val_words = load_words(vals_words, "val_words")
+        load_dealt_vector(th, TH_COL)
+        load_dealt_vector(qs, QS_COL)
+        nc.sync.dma_start(vec_rows[FADE_COL:P, :], fade.rearrange("o (b p) -> o b p", p=P).broadcast_to([8, 8, P]))
+        nc.sync.dma_start(vec_rows[SIZE_COL:FADE_COL, :], size.rearrange("o (b p) -> o b p", p=P).broadcast_to([28, 2, P]))
+        qb_raw = load_rows(query2, "qb_raw")
+        val_bytes = load_bytes(vals_scales, "val_bytes")
+        go_raw = load_rows(gout, "go_raw")
+        nc.sync.dma_start(places[:], offs4)
+        qr_raw = tile([P, PACK, D], F32, "qr_raw")
+        for r in range(PACK):
+            nc.sync.dma_start(qr_raw[:, r, :], qrows.rearrange("(c r i) d -> r c i d", r=PACK, i=RUN)[r])
+        old_sb = []
+        for h in range(2):
+            half = tile([P, 4, BANK], F32, f"old{h}")
+            nc.sync.dma_start(half[:], old[:, h * BANK:(h + 1) * BANK].rearrange("(k p) u -> p k u", p=P))
+            old_sb.append(half)
+
+        def gather(words, scale_bytes, name):
+            w = tile([P, I], U16, name + "_w")
+            s = tile([P, I], U8, name + "_s")
+            nc.vector.tensor_copy(w[:], words[:].indirect(slots[:]))
+            nc.vector.tensor_copy(s[:], scale_bytes[:].indirect(slots[:]))
+            return w, s
+
+        def deal(raw, name):
+            halves = []
+            for n in range(2):
+                grouped = sb.tile([P, Q * PACK // 2], BF16, name=f"{name}{n}", tag=f"{name}{n}", align_bytes=64)
+                src = raw[:].rearrange("p j (c r i) -> p c r j i", r=PACK, i=RUN)[:, :, 2 * n:2 * n + 2]
+                nc.vector.tensor_copy(grouped[:].rearrange("p (r c i j) -> p c r j i", r=2, i=RUN, j=PACK), src)
+                halves.append(grouped)
+            return halves
+
+        def quantize_halves(halves, name):
+            codes = tile([P, Q], U32, name + "_c")
+            scales = tile([P, Q], U8, name + "_s")
+            for n in range(2):
+                cols = slice(n * Q // 2, (n + 1) * Q // 2)
+                nc.vector.quantize_mx(out=codes[:, cols].bitcast(FP8X4), scales=scales[:, cols], in_=halves[n][:])
+            return codes, scales
+
+        def quantize(grouped, width, name):
+            codes = tile([P, width], U32, name + "_c")
+            scales = tile([P, width], U8, name + "_s")
+            nc.vector.quantize_mx(out=codes[:].bitcast(FP8X4), scales=scales[:], in_=grouped[:])
+            return codes, scales
+
+        def pair(first_bank, r):
+            return banks[first_bank + r // 2][:, (r % 2) * I:(r % 2 + 1) * I]
+
+        def scores(q_mx, first_bank):
+            for r in range(PACK):
+                cols = slice(r * P, (r + 1) * P)
+                nc.tensor.matmul_mx(out=pair(first_bank, r), lhsT=q_mx[0][:, cols].bitcast(FP8X4), lhsT_scale=q_mx[1][:, cols],
+                                    rhs=key_w[:].bitcast(FP4X4), rhs_scale=key_s[:], start=True, stop=True)
+
+        key_w, key_s = gather(key_words, key_bytes, "key")
+        qa_mx = quantize_halves(deal(qa_raw, "qa_g"), "qa")
+        val_w, val_s = gather(val_words, val_bytes, "val")
+        scores(qa_mx, 0)
+        qb_g = deal(qb_raw, "qb_g")
+
+        vec_cols = tile([P, FADE_COL + 8], F32, "vec_cols")
+        neg_th = tile([P, PACK], F32, "neg_th")
+        nc.tensor.transpose(banks[6][:, 0:P], vec_rows[:], ident[:])
+        nc.scalar.copy(vec_cols[:], banks[6][:, 0:FADE_COL + 8])
+        nc.scalar.activation(neg_th[:], banks[6][:, TH_COL:TH_COL + PACK], ACT.Copy, scale=-1.0)
+
+        qb_mx = quantize_halves(qb_g, "qb")
+        scores(qb_mx, 2)
+        go_g = deal(go_raw, "go_g")
+        ua = [tile([P, I], F32, f"ua{r}") for r in range(PACK)]
+        vb = [tile([P, I], F32, f"vb{r}") for r in range(PACK)]
+        for r in range(PACK):
+            nc.scalar.activation(ua[r][:], pair(0, r), ACT.Sigmoid, bias=neg_th[:, r:r + 1], scale=1.0)
+        for r in range(PACK):
+            nc.scalar.activation(vb[r][:], pair(2, r), ACT.Sigmoid, bias=vec_cols[:, TH_COL + r:TH_COL + r + 1], scale=-1.0)
+        go_mx = quantize_halves(go_g, "go")
+
+        sized = [[tile([P, I], F32, f"sized{n}{h}") for h in range(2)] for n in range(2)]
+        for n in range(2):
+            rows = slice(n * I, (n + 1) * I)
+            for h in range(2):
+                cols = slice(h * P, (h + 1) * P)
+                nc.tensor.matmul_mx(out=banks[4 + n][:, h * I:(h + 1) * I], lhsT=val_w[:, cols].bitcast(FP4X4), lhsT_scale=val_s[:, cols],
+                                    rhs=go_mx[0][:, rows].bitcast(FP8X4), rhs_scale=go_mx[1][:, rows], start=True, stop=True)
+        for n in range(2):
+            for h in range(2):
+                nc.scalar.activation(sized[n][h][:], banks[4 + n][:, h * I:(h + 1) * I], ACT.Copy,
+                                     scale=vec_cols[:, SIZE_COL + h:SIZE_COL + h + 1])
+            for r in (2 * n, 2 * n + 1):
+                for h in range(2):
+                    nc.tensor.transpose(pair(6, r)[:, h * P:(h + 1) * P], sized[n][h][:, (r % 2) * P:(r % 2 + 1) * P], ident[:])
+
+        neg_m_pairs = [sb.tile([P, 2 * I], F32, name=f"neg_m{n}", tag=f"go_g{1 - n}", align_bytes=64) for n in range(2)]
+        neg_m = [neg_m_pairs[r // 2][:, (r % 2) * I:(r % 2 + 1) * I] for r in range(PACK)]
+        neg_m_sum = tile([P, PACK], F32, "neg_m_sum")
+        for r in range(PACK):
+            nc.vector.scalar_tensor_tensor(neg_m[r], ua[r][:], 1.0, vb[r][:], ALU.subtract, ALU.mult,
+                                           accum_out=neg_m_sum[:, r:r + 1])
+        z = tile([P, PACK], F32, "z")
+        inv_z = tile([P, PACK], F32, "inv_z")
+        factor = tile([P, PACK], F32, "factor")
+        nc.vector.tensor_scalar(z[:], neg_m_sum[:], float(I), None, ALU.add)
+        nc.vector.reciprocal(inv_z[:], z[:])
+        nc.vector.scalar_tensor_tensor(factor[:], inv_z[:], -1.0, vec_cols[:, QS_COL:QS_COL + PACK], ALU.mult, ALU.mult)
+        ua_scaled = tile([P, PACK * I], F32, "ua_scaled")
+        for r in range(PACK):
+            nc.gpsimd.tensor_scalar(ua_scaled[:, r * I:(r + 1) * I], ua[r][:], factor[:, r:r + 1], 0.0, ALU.mult, ALU.add)
+        weighted = [tile([P, I], F32, f"weighted{n}") for n in range(2)]
+        wsum = [tile([P, 1], F32, f"wsum{r}") for r in range(PACK)]
+        mean = [tile([P, 1], F32, f"mean{r}") for r in range(PACK)]
+        for r in range(PACK):
+            nc.vector.scalar_tensor_tensor(weighted[r % 2][:], neg_m[r], 1.0, pair(6, r), ALU.add, ALU.mult,
+                                           accum_out=wsum[r][:])
+        for r in range(PACK):
+            nc.vector.tensor_scalar(mean[r][:], wsum[r][:], inv_z[:, r:r + 1], None, ALU.mult)
+
+        qr_g = tile([P, D * PACK], BF16, "qr_g")
+        for n in range(2):
+            nc.scalar.copy(qr_g[:, n * 1024:(n + 1) * 1024].rearrange("p (c i r) -> p c r i", i=RUN, r=PACK),
+                           qr_raw[:, :, n * 256:(n + 1) * 256].rearrange("p r (c i) -> p c r i", i=RUN))
+
+        faded = [tile([P, D], F32, f"faded{b}") for b in range(8)]
+
+        def fade_block(b):
+            bank = banks[FADE_BANK[b]]
+            for k in range(4):
+                nc.tensor.transpose(bank[:, k * P:(k + 1) * P], old_sb[b // 4][:, k, (b % 4) * P:(b % 4 + 1) * P], ident[:])
+            nc.scalar.activation(faded[b][:], bank[:], ACT.Copy, scale=vec_cols[:, FADE_COL + b:FADE_COL + b + 1])
+
+        back = {}
+
+        def turn_back(k, h):
+            bank = banks[BACK_BANK[h][k]]
+            for c in range(4):
+                nc.tensor.transpose(bank[:, c * P:(c + 1) * P], faded[4 * h + c][:, k * P:(k + 1) * P], ident[:])
+            if (k, h) in ON_GPSIMD:
+                staged = tile([P, BANK], F32, f"staged{k}{h}")
+                nc.scalar.copy(staged[:], bank[:])
+                back[k, h] = staged
+            else:
+                back[k, h] = bank
+
+        def add_and_store(k, h):
+            cols = slice(h * BANK, (h + 1) * BANK)
+            result = tile([P, BANK], F32, f"result{k}{h}")
+            engine = nc.gpsimd if (k, h) in ON_GPSIMD else nc.vector
+            engine.tensor_tensor(result[:], back[k, h][:], placed[k][:, cols], ALU.add)
+            nc.sync.dma_start(out[k * P:(k + 1) * P, cols], result[:])
+
+        for b in range(4):
+            fade_block(b)
+        turn_back(0, 0)
+        turn_back(1, 0)
+
+        centred = tile([P, PACK * I], F32, "centred")
+        for r in range(PACK):
+            nc.vector.scalar_tensor_tensor(centred[:, r * I:(r + 1) * I], pair(6, r), mean[r][:], neg_m[r],
+                                           ALU.subtract, ALU.mult)
+        gs_g = tile([P, I * PACK], BF16, "gs_g")
+        gs_codes = tile([P, I], U32, "gs_codes")
+        gs_scales = tile([P, I], U8, "gs_scales")
+
+        def by_runs(t, pattern):
+            return t[:].rearrange(pattern, i=RUN, r=PACK)
+
+        def finish_gs(n):
+            c = slice(n * 32, (n + 1) * 32)
+            nc.vector.tensor_tensor(by_runs(gs_g, "p (c i r) -> p c r i")[:, c], by_runs(centred, "p (r c i) -> p c r i")[:, c],
+                                    by_runs(ua_scaled, "p (r c i) -> p c r i")[:, c], ALU.mult)
+
+        def quantize_gs(n):
+            cols = slice(n * P, (n + 1) * P)
+            nc.vector.quantize_mx(out=gs_codes[:, cols].bitcast(FP8X4), scales=gs_scales[:, cols],
+                                  in_=gs_g[:, n * P * PACK:(n + 1) * P * PACK])
+
+        def key_gradient(k, first, last, tag):
+            cols = slice(k * P, (k + 1) * P)
+            nc.tensor.matmul_mx(out=banks[4 + k][:, first:last], lhsT=qr_mx[0][:, cols].bitcast(FP8X4), lhsT_scale=qr_mx[1][:, cols],
+                                rhs=gs_codes[:, first:last].bitcast(FP8X4), rhs_scale=gs_scales[:, first:last], start=True, stop=True)
+            gk = sb.tile([P, last - first], F32, name=f"gk{k}_{first}", tag=tag)
+            nc.scalar.copy(gk[:], banks[4 + k][:, first:last])
+            return gk
+
+        def place(k, first, last, gk):
+            nc.vector.tensor_copy(placed[k][:].indirect(places[:, first // 16:last // 16]), gk[:])
+
+        finish_gs(0)
+        qr_mx = quantize(qr_g, D, "qr")
+        quantize_gs(0)
+        finish_gs(1)
+        early = [key_gradient(k, 0, P, f"gk_early{k}") for k in range(2)]
+        quantize_gs(1)
+        for k in range(2):
+            place(k, 0, P, early[k])
+        for k in range(2):
+            place(k, P, I, key_gradient(k, P, I, f"gk_late{k}"))
+        for k in range(2, 4):
+            place(k, 0, I, key_gradient(k, 0, I, f"gk_late{k}"))
+        for b in range(4, 8):
+            fade_block(b)
+        turn_back(2, 0)
+        turn_back(3, 0)
+        for k, h in ADD_ORDER:
+            if h == 1:
+                turn_back(k, h)
+            add_and_store(k, h)

@@ -20,11 +20,9 @@ RUN = 4
 D, E, T, I, Q, U = 512, 512, 1024, 256, 512, 1024
 BANK = 512
 FLOPS = 2 * Q * I * (D + D + E + D)
-FADE_BANK = (0, 1, 2, 3, 2, 3, 4, 5)
-BACK_BANK = ((0, 1, 6, 7), (2, 3, 4, 5))
-ON_GPSIMD = ()
-ADD_ORDER = ((0, 0), (1, 0), (2, 0), (3, 0), (0, 1), (1, 1), (2, 1), (3, 1))
-TH_COL, QS_COL, SIZE_COL, FADE_COL = 0, 4, 8, 64
+GK_BANK = (4, 5, 6, 7)
+FADE_BANK = (4, 5, 6, 4)
+FADE_COL, SIZE_COL, VEC_COLS = 0, 8, 16
 
 
 def tile_attend_beitherquestion_k_kernel(tc, query, query2, keys_words, keys_scales, th, gout, vals_words, vals_scales,
@@ -35,11 +33,15 @@ def tile_attend_beitherquestion_k_kernel(tc, query, query2, keys_words, keys_sca
         ps = ctx.enter_context(tc.psum_pool(name="ps", bufs=1))
 
         def tile(shape, dtype, name):
-            return sb.tile(shape, dtype, name=name, align_bytes=64)
+            return sb.tile(shape, dtype, name=name, tag=name, align_bytes=64)
 
         banks = [ps.tile([P, BANK], F32, name=f"bank{b}") for b in range(8)]
 
         vec_rows = tile([P, P], F32, "vec_rows")
+        nc.vector.memset(vec_rows[:], 0.0)
+        zeroed = {name: tile([P, T], U8, name) for name in ("key_bytes", "val_bytes")}
+        nc.gpsimd.memset(zeroed["key_bytes"][:].bitcast(I32), 0)
+        nc.vector.memset(zeroed["val_bytes"][:].bitcast(I32), 0)
         placed = [tile([P, U], F32, f"placed{k}") for k in range(4)]
         for k in range(4):
             nc.vector.memset(placed[k][:], 0.0)
@@ -56,11 +58,10 @@ def tile_attend_beitherquestion_k_kernel(tc, query, query2, keys_words, keys_sca
             return words
 
         def load_bytes(src, name):
-            scale_bytes = tile([P, T], U8, name)
+            scale_bytes = zeroed[name]
+            rows = src[0].rearrange("(g r) t -> g r t", r=4)
             for g in range(4):
-                rows = src[0, 4 * g:4 * g + 4, :].bitcast(I32)
-                nc.sync.dma_start(scale_bytes[32 * g:32 * g + 32, :].bitcast(I32),
-                                  rows.unsqueeze(0).broadcast_to([8, 4, T // 4]))
+                nc.sync.dma_start(scale_bytes[32 * g:32 * g + 4, :].bitcast(I32), rows[g].bitcast(I32))
             return scale_bytes
 
         def load_rows(src, name):
@@ -68,28 +69,27 @@ def tile_attend_beitherquestion_k_kernel(tc, query, query2, keys_words, keys_sca
             nc.sync.dma_start(raw[:], src.rearrange("(p j) w -> p j w", j=PACK))
             return raw
 
-        def load_dealt_vector(src, first):
-            nc.sync.dma_start(vec_rows[first:first + PACK, :].rearrange("r (c i) -> r c i", i=RUN),
-                              src.rearrange("(c r i) o -> r c (i o)", r=PACK, i=RUN))
+        def load_row_vector(src, name):
+            cols = tile([P, PACK], F32, name)
+            nc.sync.dma_start(cols[:], src.rearrange("(p r) o -> p (r o)", r=PACK))
+            return cols
 
         slots = sb.tile([P, I // 16], U16, name="slots")
         places = sb.tile([P, I // 16], U16, name="places")
         nc.sync.dma_start(slots[:], offs)
+        th_sb = load_row_vector(th, "th_sb")
         key_words = load_words(keys_words, "key_words")
         key_bytes = load_bytes(keys_scales, "key_bytes")
         qa_raw = load_rows(query, "qa_raw")
         val_words = load_words(vals_words, "val_words")
-        load_dealt_vector(th, TH_COL)
-        load_dealt_vector(qs, QS_COL)
-        nc.sync.dma_start(vec_rows[FADE_COL:P, :], fade.rearrange("o (b p) -> o b p", p=P).broadcast_to([8, 8, P]))
-        nc.sync.dma_start(vec_rows[SIZE_COL:FADE_COL, :], size.rearrange("o (b p) -> o b p", p=P).broadcast_to([28, 2, P]))
         qb_raw = load_rows(query2, "qb_raw")
         val_bytes = load_bytes(vals_scales, "val_bytes")
         go_raw = load_rows(gout, "go_raw")
+        nc.sync.dma_start(vec_rows[SIZE_COL:SIZE_COL + 2, :], size.rearrange("o (b p) -> (o b) p", p=P))
+        nc.sync.dma_start(vec_rows[FADE_COL:FADE_COL + 8, :], fade.rearrange("o (b p) -> (o b) p", p=P))
+        qs_sb = load_row_vector(qs, "qs_sb")
         nc.sync.dma_start(places[:], offs4)
-        qr_raw = tile([P, PACK, D], F32, "qr_raw")
-        for r in range(PACK):
-            nc.sync.dma_start(qr_raw[:, r, :], qrows.rearrange("(c r i) d -> r c i d", r=PACK, i=RUN)[r])
+        qr_raw = load_rows(qrows, "qr_raw")
         old_sb = []
         for h in range(2):
             half = tile([P, 4, BANK], F32, f"old{h}")
@@ -107,8 +107,8 @@ def tile_attend_beitherquestion_k_kernel(tc, query, query2, keys_words, keys_sca
             halves = []
             for n in range(2):
                 grouped = sb.tile([P, Q * PACK // 2], BF16, name=f"{name}{n}", tag=f"{name}{n}", align_bytes=64)
-                src = raw[:].rearrange("p j (c r i) -> p c r j i", r=PACK, i=RUN)[:, :, 2 * n:2 * n + 2]
-                nc.vector.tensor_copy(grouped[:].rearrange("p (r c i j) -> p c r j i", r=2, i=RUN, j=PACK), src)
+                src = raw[:].rearrange("p j (s r) -> p s j r", r=PACK)[:, :, :, 2 * n:2 * n + 2]
+                nc.vector.tensor_copy(grouped[:].rearrange("p (r s j) -> p s j r", r=2, j=PACK), src)
                 halves.append(grouped)
             return halves
 
@@ -120,12 +120,6 @@ def tile_attend_beitherquestion_k_kernel(tc, query, query2, keys_words, keys_sca
                 nc.vector.quantize_mx(out=codes[:, cols].bitcast(FP8X4), scales=scales[:, cols], in_=halves[n][:])
             return codes, scales
 
-        def quantize(grouped, width, name):
-            codes = tile([P, width], U32, name + "_c")
-            scales = tile([P, width], U8, name + "_s")
-            nc.vector.quantize_mx(out=codes[:].bitcast(FP8X4), scales=scales[:], in_=grouped[:])
-            return codes, scales
-
         def pair(first_bank, r):
             return banks[first_bank + r // 2][:, (r % 2) * I:(r % 2 + 1) * I]
 
@@ -135,17 +129,13 @@ def tile_attend_beitherquestion_k_kernel(tc, query, query2, keys_words, keys_sca
                 nc.tensor.matmul_mx(out=pair(first_bank, r), lhsT=q_mx[0][:, cols].bitcast(FP8X4), lhsT_scale=q_mx[1][:, cols],
                                     rhs=key_w[:].bitcast(FP4X4), rhs_scale=key_s[:], start=True, stop=True)
 
+        neg_th = tile([P, PACK], F32, "neg_th")
+        nc.vector.tensor_scalar(neg_th[:], th_sb[:], -1.0, None, ALU.mult)
         key_w, key_s = gather(key_words, key_bytes, "key")
         qa_mx = quantize_halves(deal(qa_raw, "qa_g"), "qa")
         val_w, val_s = gather(val_words, val_bytes, "val")
         scores(qa_mx, 0)
         qb_g = deal(qb_raw, "qb_g")
-
-        vec_cols = tile([P, FADE_COL + 8], F32, "vec_cols")
-        neg_th = tile([P, PACK], F32, "neg_th")
-        nc.tensor.transpose(banks[6][:, 0:P], vec_rows[:], ident[:])
-        nc.scalar.copy(vec_cols[:], banks[6][:, 0:FADE_COL + 8])
-        nc.scalar.activation(neg_th[:], banks[6][:, TH_COL:TH_COL + PACK], ACT.Copy, scale=-1.0)
 
         qb_mx = quantize_halves(qb_g, "qb")
         scores(qb_mx, 2)
@@ -155,9 +145,12 @@ def tile_attend_beitherquestion_k_kernel(tc, query, query2, keys_words, keys_sca
         for r in range(PACK):
             nc.scalar.activation(ua[r][:], pair(0, r), ACT.Sigmoid, bias=neg_th[:, r:r + 1], scale=1.0)
         for r in range(PACK):
-            nc.scalar.activation(vb[r][:], pair(2, r), ACT.Sigmoid, bias=vec_cols[:, TH_COL + r:TH_COL + r + 1], scale=-1.0)
+            nc.scalar.activation(vb[r][:], pair(2, r), ACT.Sigmoid, bias=th_sb[:, r:r + 1], scale=-1.0)
         go_mx = quantize_halves(go_g, "go")
 
+        vec_cols = tile([P, VEC_COLS], F32, "vec_cols")
+        nc.tensor.transpose(banks[6][:, 0:P], vec_rows[:], ident[:])
+        nc.scalar.copy(vec_cols[:], banks[6][:, 0:VEC_COLS])
         sized = [[tile([P, I], F32, f"sized{n}{h}") for h in range(2)] for n in range(2)]
         for n in range(2):
             rows = slice(n * I, (n + 1) * I)
@@ -184,10 +177,10 @@ def tile_attend_beitherquestion_k_kernel(tc, query, query2, keys_words, keys_sca
         factor = tile([P, PACK], F32, "factor")
         nc.vector.tensor_scalar(z[:], neg_m_sum[:], float(I), None, ALU.add)
         nc.vector.reciprocal(inv_z[:], z[:])
-        nc.vector.scalar_tensor_tensor(factor[:], inv_z[:], -1.0, vec_cols[:, QS_COL:QS_COL + PACK], ALU.mult, ALU.mult)
+        nc.vector.scalar_tensor_tensor(factor[:], inv_z[:], -1.0, qs_sb[:], ALU.mult, ALU.mult)
         ua_scaled = tile([P, PACK * I], F32, "ua_scaled")
         for r in range(PACK):
-            nc.gpsimd.tensor_scalar(ua_scaled[:, r * I:(r + 1) * I], ua[r][:], factor[:, r:r + 1], 0.0, ALU.mult, ALU.add)
+            nc.scalar.activation(ua_scaled[:, r * I:(r + 1) * I], ua[r][:], ACT.Copy, scale=factor[:, r:r + 1])
         weighted = [tile([P, I], F32, f"weighted{n}") for n in range(2)]
         wsum = [tile([P, 1], F32, f"wsum{r}") for r in range(PACK)]
         mean = [tile([P, 1], F32, f"mean{r}") for r in range(PACK)]
@@ -197,49 +190,27 @@ def tile_attend_beitherquestion_k_kernel(tc, query, query2, keys_words, keys_sca
         for r in range(PACK):
             nc.vector.tensor_scalar(mean[r][:], wsum[r][:], inv_z[:, r:r + 1], None, ALU.mult)
 
-        qr_g = tile([P, D * PACK], BF16, "qr_g")
+        qr_g = [sb.tile([P, D * PACK // 2], BF16, name=f"qr_g{n}", tag=("sized11", "ua3")[n], align_bytes=64) for n in range(2)]
+        qr_mx = [tile([P, D], U32, "qr_c"), tile([P, D], U8, "qr_s")]
+
+        def quantize_qr(n):
+            cols = slice(n * D // 2, (n + 1) * D // 2)
+            nc.vector.quantize_mx(out=qr_mx[0][:, cols].bitcast(FP8X4), scales=qr_mx[1][:, cols], in_=qr_g[n][:])
+
         for n in range(2):
-            nc.scalar.copy(qr_g[:, n * 1024:(n + 1) * 1024].rearrange("p (c i r) -> p c r i", i=RUN, r=PACK),
+            nc.scalar.copy(qr_g[n][:].rearrange("p (c i r) -> p c r i", i=RUN, r=PACK),
                            qr_raw[:, :, n * 256:(n + 1) * 256].rearrange("p r (c i) -> p c r i", i=RUN))
 
-        faded = [tile([P, D], F32, f"faded{b}") for b in range(8)]
-
-        def fade_block(b):
-            bank = banks[FADE_BANK[b]]
-            for k in range(4):
-                nc.tensor.transpose(bank[:, k * P:(k + 1) * P], old_sb[b // 4][:, k, (b % 4) * P:(b % 4 + 1) * P], ident[:])
-            nc.scalar.activation(faded[b][:], bank[:], ACT.Copy, scale=vec_cols[:, FADE_COL + b:FADE_COL + b + 1])
-
-        back = {}
-
-        def turn_back(k, h):
-            bank = banks[BACK_BANK[h][k]]
-            for c in range(4):
-                nc.tensor.transpose(bank[:, c * P:(c + 1) * P], faded[4 * h + c][:, k * P:(k + 1) * P], ident[:])
-            if (k, h) in ON_GPSIMD:
-                staged = tile([P, BANK], F32, f"staged{k}{h}")
-                nc.scalar.copy(staged[:], bank[:])
-                back[k, h] = staged
-            else:
-                back[k, h] = bank
-
-        def add_and_store(k, h):
-            cols = slice(h * BANK, (h + 1) * BANK)
-            result = tile([P, BANK], F32, f"result{k}{h}")
-            engine = nc.gpsimd if (k, h) in ON_GPSIMD else nc.vector
-            engine.tensor_tensor(result[:], back[k, h][:], placed[k][:, cols], ALU.add)
-            nc.sync.dma_start(out[k * P:(k + 1) * P, cols], result[:])
-
+        fade_wide = tile([P, BANK], F32, "fade_wide")
         for b in range(4):
-            fade_block(b)
-        turn_back(0, 0)
-        turn_back(1, 0)
+            nc.tensor.transpose(banks[0][:, b * P:(b + 1) * P], vec_cols[:, FADE_COL + b:FADE_COL + b + 1].to_broadcast([P, P]), ident[:])
+        nc.scalar.copy(fade_wide[:], banks[0][:])
 
         centred = tile([P, PACK * I], F32, "centred")
         for r in range(PACK):
             nc.vector.scalar_tensor_tensor(centred[:, r * I:(r + 1) * I], pair(6, r), mean[r][:], neg_m[r],
                                            ALU.subtract, ALU.mult)
-        gs_g = tile([P, I * PACK], BF16, "gs_g")
+        gs_g = [tile([P, P * PACK], BF16, f"gs_g{n}") for n in range(2)]
         gs_codes = tile([P, I], U32, "gs_codes")
         gs_scales = tile([P, I], U8, "gs_scales")
 
@@ -248,42 +219,86 @@ def tile_attend_beitherquestion_k_kernel(tc, query, query2, keys_words, keys_sca
 
         def finish_gs(n):
             c = slice(n * 32, (n + 1) * 32)
-            nc.vector.tensor_tensor(by_runs(gs_g, "p (c i r) -> p c r i")[:, c], by_runs(centred, "p (r c i) -> p c r i")[:, c],
+            nc.vector.tensor_tensor(by_runs(gs_g[n], "p (c i r) -> p c r i"), by_runs(centred, "p (r c i) -> p c r i")[:, c],
                                     by_runs(ua_scaled, "p (r c i) -> p c r i")[:, c], ALU.mult)
 
         def quantize_gs(n):
             cols = slice(n * P, (n + 1) * P)
             nc.vector.quantize_mx(out=gs_codes[:, cols].bitcast(FP8X4), scales=gs_scales[:, cols],
-                                  in_=gs_g[:, n * P * PACK:(n + 1) * P * PACK])
+                                  in_=gs_g[n][:])
 
         def key_gradient(k, first, last, tag):
             cols = slice(k * P, (k + 1) * P)
-            nc.tensor.matmul_mx(out=banks[4 + k][:, first:last], lhsT=qr_mx[0][:, cols].bitcast(FP8X4), lhsT_scale=qr_mx[1][:, cols],
+            nc.tensor.matmul_mx(out=banks[GK_BANK[k]][:, first:last], lhsT=qr_mx[0][:, cols].bitcast(FP8X4), lhsT_scale=qr_mx[1][:, cols],
                                 rhs=gs_codes[:, first:last].bitcast(FP8X4), rhs_scale=gs_scales[:, first:last], start=True, stop=True)
-            gk = sb.tile([P, last - first], F32, name=f"gk{k}_{first}", tag=tag)
-            nc.scalar.copy(gk[:], banks[4 + k][:, first:last])
+            gk = sb.tile([P, last - first], F32, name=f"gk{k}_{first}", tag=tag, align_bytes=64)
+            nc.scalar.copy(gk[:], banks[GK_BANK[k]][:, first:last])
             return gk
 
         def place(k, first, last, gk):
             nc.vector.tensor_copy(placed[k][:].indirect(places[:, first // 16:last // 16]), gk[:])
 
         finish_gs(0)
-        qr_mx = quantize(qr_g, D, "qr")
+        quantize_qr(0)
         quantize_gs(0)
         finish_gs(1)
         early = [key_gradient(k, 0, P, f"gk_early{k}") for k in range(2)]
         quantize_gs(1)
+        quantize_qr(1)
         for k in range(2):
             place(k, 0, P, early[k])
         for k in range(2):
             place(k, P, I, key_gradient(k, P, I, f"gk_late{k}"))
-        for k in range(2, 4):
-            place(k, 0, I, key_gradient(k, 0, I, f"gk_late{k}"))
-        for b in range(4, 8):
-            fade_block(b)
-        turn_back(2, 0)
-        turn_back(3, 0)
-        for k, h in ADD_ORDER:
-            if h == 1:
-                turn_back(k, h)
-            add_and_store(k, h)
+        place(2, 0, I, key_gradient(2, 0, I, "gk_late2"))
+
+        def store(k, h, result):
+            nc.sync.dma_start(out[k * P:(k + 1) * P, h * BANK:(h + 1) * BANK], result[:])
+
+        products = sb.tile([P, 3 * BANK], F32, name="products", tag="ua3", align_bytes=64)
+
+        def gpsimd_fade(k):
+            nc.gpsimd.tensor_tensor(products[:, k * BANK:(k + 1) * BANK], old_sb[0][:, k, :], fade_wide[:], ALU.mult)
+
+        def gpsimd_add(k):
+            result = tile([P, BANK], F32, f"result{k}0")
+            nc.gpsimd.tensor_tensor(result[:], products[:, k * BANK:(k + 1) * BANK], placed[k][:, 0:BANK], ALU.add)
+            store(k, 0, result)
+
+        def vector_add(k, h, bank):
+            result = tile([P, BANK], F32, f"result{k}{h}")
+            nc.vector.tensor_tensor(result[:], bank[:], placed[k][:, h * BANK:(h + 1) * BANK], ALU.add)
+            store(k, h, result)
+
+        gpsimd_fade(0)
+        gpsimd_fade(1)
+        gpsimd_add(0)
+        gpsimd_add(1)
+        gpsimd_fade(2)
+        gpsimd_add(2)
+
+        faded = [tile([P, D], F32, f"faded{c}") for c in range(4)]
+        for c in range(4):
+            for k in range(4):
+                nc.tensor.transpose(banks[FADE_BANK[c]][:, k * P:(k + 1) * P], old_sb[1][:, k, c * P:(c + 1) * P], ident[:])
+            nc.scalar.activation(faded[c][:], banks[FADE_BANK[c]][:], ACT.Copy, scale=vec_cols[:, FADE_COL + 4 + c:FADE_COL + 5 + c])
+
+        def turn_back(k, bank):
+            for c in range(4):
+                nc.tensor.transpose(bank[:, c * P:(c + 1) * P], faded[c][:, k * P:(k + 1) * P], ident[:])
+
+        for k in range(4):
+            turn_back(k, banks[k])
+        last_gk = key_gradient(3, 0, I, "faded3")
+        for k in range(3):
+            vector_add(k, 1, banks[k])
+        place(3, 0, I, last_gk)
+        corner = [tile([P, P], F32, f"corner{c}") for c in range(4)]
+        for c in range(4):
+            nc.tensor.transpose(banks[5][:, c * P:(c + 1) * P], old_sb[0][:, 3, c * P:(c + 1) * P], ident[:])
+        for c in range(4):
+            nc.scalar.activation(corner[c][:], banks[5][:, c * P:(c + 1) * P], ACT.Copy,
+                                 scale=vec_cols[:, FADE_COL + c:FADE_COL + c + 1])
+        for c in range(4):
+            nc.tensor.transpose(banks[6][:, c * P:(c + 1) * P], corner[c][:], ident[:])
+        vector_add(3, 0, banks[6])
+        vector_add(3, 1, banks[3])

@@ -47,10 +47,6 @@ def tile_attend_beitherquestion_k_kernel(tc, query, query2, keys_words, keys_sca
             nc.vector.memset(placed[k][:], 0.0)
         ident = tile([P, P], F32, "ident")
         make_identity(nc, ident[:])
-        warm_in = tile([P, 1], F32, "warm_in")
-        warm_out = tile([P, 1], F32, "warm_out")
-        nc.gpsimd.memset(warm_in[:], 0.0)
-        nc.scalar.activation(warm_out[:], warm_in[:], ACT.Sigmoid)
 
         def load_words(src, name):
             words = tile([P, T], U16, name)
@@ -251,8 +247,10 @@ def tile_attend_beitherquestion_k_kernel(tc, query, query2, keys_words, keys_sca
             place(k, P, I, key_gradient(k, P, I, f"gk_late{k}"))
         place(2, 0, I, key_gradient(2, 0, I, "gk_late2"))
 
-        def store(k, h, result):
-            nc.sync.dma_start(out[k * P:(k + 1) * P, h * BANK:(h + 1) * BANK], result[:])
+        results = [tile([P, U], F32, f"result{k}") for k in range(4)]
+
+        def store(k, first, last):
+            nc.sync.dma_start(out[k * P:(k + 1) * P, first:last], results[k][:, first:last])
 
         products = sb.tile([P, 3 * BANK], F32, name="products", tag="ua3", align_bytes=64)
 
@@ -260,19 +258,17 @@ def tile_attend_beitherquestion_k_kernel(tc, query, query2, keys_words, keys_sca
             nc.gpsimd.tensor_tensor(products[:, k * BANK:(k + 1) * BANK], old_sb[0][:, k, :], fade_wide[:], ALU.mult)
 
         def gpsimd_add(k):
-            result = tile([P, BANK], F32, f"result{k}0")
-            nc.gpsimd.tensor_tensor(result[:], products[:, k * BANK:(k + 1) * BANK], placed[k][:, 0:BANK], ALU.add)
-            store(k, 0, result)
+            nc.gpsimd.tensor_tensor(results[k][:, 0:BANK], products[:, k * BANK:(k + 1) * BANK], placed[k][:, 0:BANK], ALU.add)
 
         def vector_add(k, h, bank):
-            result = tile([P, BANK], F32, f"result{k}{h}")
-            nc.vector.tensor_tensor(result[:], bank[:], placed[k][:, h * BANK:(h + 1) * BANK], ALU.add)
-            store(k, h, result)
+            cols = slice(h * BANK, (h + 1) * BANK)
+            nc.vector.tensor_tensor(results[k][:, cols], bank[:], placed[k][:, cols], ALU.add)
 
         gpsimd_fade(0)
         gpsimd_fade(1)
-        gpsimd_add(0)
-        gpsimd_add(1)
+        for k in range(2):
+            gpsimd_add(k)
+            store(k, 0, BANK)
         gpsimd_fade(2)
         gpsimd_add(2)
 
@@ -291,6 +287,7 @@ def tile_attend_beitherquestion_k_kernel(tc, query, query2, keys_words, keys_sca
         last_gk = key_gradient(3, 0, I, "faded3")
         for k in range(3):
             vector_add(k, 1, banks[k])
+            store(k, 0 if k == 2 else BANK, U)
         place(3, 0, I, last_gk)
         corner = [tile([P, P], F32, f"corner{c}") for c in range(4)]
         for c in range(4):
@@ -301,4 +298,6 @@ def tile_attend_beitherquestion_k_kernel(tc, query, query2, keys_words, keys_sca
         for c in range(4):
             nc.tensor.transpose(banks[6][:, c * P:(c + 1) * P], corner[c][:], ident[:])
         vector_add(3, 0, banks[6])
+        store(3, 0, BANK)
         vector_add(3, 1, banks[3])
+        store(3, BANK, U)

from contextlib import ExitStack

import concourse.mybir as mybir
from concourse.masks import make_identity

F32 = mybir.dt.float32
BF16 = mybir.dt.bfloat16
I32 = mybir.dt.int32
U32 = mybir.dt.uint32
U16 = mybir.dt.uint16
U8 = mybir.dt.uint8
FP8X4 = mybir.dt.float8_e4m3fn_x4
FP4X4 = mybir.dt.float4_e2m1fn_x4
ALU = mybir.AluOpType
ACT = mybir.ActivationFunctionType

P = 128
PACK = 4
RUN = 4
D, E, T, I, Q, U = 512, 512, 1024, 256, 512, 1024
BANK = 512
FLOPS = 2 * Q * I * (D + D + E + D)
GK_BANK = (4, 5, 6, 7)
FADE_BANK = (4, 5, 6, 4)
FADE_COL, SIZE_COL, VEC_COLS = 0, 8, 16


def tile_attend_beitherquestion_k_kernel(tc, query, query2, keys_words, keys_scales, th, gout, vals_words, vals_scales,
                                          size, qs, qrows, old, fade, offs, offs4, out):
    nc = tc.nc
    with ExitStack() as ctx:
        sb = ctx.enter_context(tc.tile_pool(name="sb", bufs=1))
        ps = ctx.enter_context(tc.psum_pool(name="ps", bufs=1))

        def tile(shape, dtype, name):
            return sb.tile(shape, dtype, name=name, tag=name, align_bytes=64)

        banks = [ps.tile([P, BANK], F32, name=f"bank{b}") for b in range(8)]

        vec_rows = tile([P, P], F32, "vec_rows")
        nc.vector.memset(vec_rows[:], 0.0)
        zeroed = {name: tile([P, T], U8, name) for name in ("key_bytes", "val_bytes")}
        nc.gpsimd.memset(zeroed["key_bytes"][:].bitcast(I32), 0)
        nc.vector.memset(zeroed["val_bytes"][:].bitcast(I32), 0)
        placed = [tile([P, U], F32, f"placed{k}") for k in range(4)]
        for k in range(4):
            nc.vector.memset(placed[k][:], 0.0)
        ident = tile([P, P], F32, "ident")
        make_identity(nc, ident[:])

        def load_words(src, name):
            words = tile([P, T], U16, name)
            nc.sync.dma_start(words[:].bitcast(I32), src[0].bitcast(I32))
            return words

        def load_bytes(src, name):
            scale_bytes = zeroed[name]
            rows = src[0].rearrange("(g r) t -> g r t", r=4)
            for g in range(4):
                nc.sync.dma_start(scale_bytes[32 * g:32 * g + 4, :].bitcast(I32), rows[g].bitcast(I32))
            return scale_bytes

        def load_rows(src, name):
            raw = tile([P, PACK, Q], F32, name)
            nc.sync.dma_start(raw[:], src.rearrange("(p j) w -> p j w", j=PACK))
            return raw

        def load_row_vector(src, name):
            cols = tile([P, PACK], F32, name)
            nc.sync.dma_start(cols[:], src.rearrange("(p r) o -> p (r o)", r=PACK))
            return cols

        slots = sb.tile([P, I // 16], U16, name="slots")
        places = sb.tile([P, I // 16], U16, name="places")
        nc.sync.dma_start(slots[:], offs)
        th_sb = load_row_vector(th, "th_sb")
        key_words = load_words(keys_words, "key_words")
        key_bytes = load_bytes(keys_scales, "key_bytes")
        qa_raw = load_rows(query, "qa_raw")
        val_words = load_words(vals_words, "val_words")
        qb_raw = load_rows(query2, "qb_raw")
        val_bytes = load_bytes(vals_scales, "val_bytes")
        go_raw = load_rows(gout, "go_raw")
        nc.sync.dma_start(vec_rows[SIZE_COL:SIZE_COL + 2, :], size.rearrange("o (b p) -> (o b) p", p=P))
        nc.sync.dma_start(vec_rows[FADE_COL:FADE_COL + 8, :], fade.rearrange("o (b p) -> (o b) p", p=P))
        qs_sb = load_row_vector(qs, "qs_sb")
        nc.sync.dma_start(places[:], offs4)
        qr_raw = load_rows(qrows, "qr_raw")
        old_sb = []
        for h in range(2):
            half = tile([P, 4, BANK], F32, f"old{h}")
            nc.sync.dma_start(half[:], old[:, h * BANK:(h + 1) * BANK].rearrange("(k p) u -> p k u", p=P))
            old_sb.append(half)

        def gather(words, scale_bytes, name):
            w = tile([P, I], U16, name + "_w")
            s = tile([P, I], U8, name + "_s")
            nc.vector.tensor_copy(w[:], words[:].indirect(slots[:]))
            nc.vector.tensor_copy(s[:], scale_bytes[:].indirect(slots[:]))
            return w, s

        def deal(raw, name):
            halves = []
            for n in range(2):
                grouped = sb.tile([P, Q * PACK // 2], BF16, name=f"{name}{n}", tag=f"{name}{n}", align_bytes=64)
                src = raw[:].rearrange("p j (s r) -> p s j r", r=PACK)[:, :, :, 2 * n:2 * n + 2]
                nc.vector.tensor_copy(grouped[:].rearrange("p (r s j) -> p s j r", r=2, j=PACK), src)
                halves.append(grouped)
            return halves

        def quantize_halves(halves, name):
            codes = tile([P, Q], U32, name + "_c")
            scales = tile([P, Q], U8, name + "_s")
            for n in range(2):
                cols = slice(n * Q // 2, (n + 1) * Q // 2)
                nc.vector.quantize_mx(out=codes[:, cols].bitcast(FP8X4), scales=scales[:, cols], in_=halves[n][:])
            return codes, scales

        def pair(first_bank, r):
            return banks[first_bank + r // 2][:, (r % 2) * I:(r % 2 + 1) * I]

        def scores(q_mx, first_bank):
            for r in range(PACK):
                cols = slice(r * P, (r + 1) * P)
                nc.tensor.matmul_mx(out=pair(first_bank, r), lhsT=q_mx[0][:, cols].bitcast(FP8X4), lhsT_scale=q_mx[1][:, cols],
                                    rhs=key_w[:].bitcast(FP4X4), rhs_scale=key_s[:], start=True, stop=True)

        neg_th = tile([P, PACK], F32, "neg_th")
        nc.vector.tensor_scalar(neg_th[:], th_sb[:], -1.0, None, ALU.mult)
        key_w, key_s = gather(key_words, key_bytes, "key")
        qa_mx = quantize_halves(deal(qa_raw, "qa_g"), "qa")
        val_w, val_s = gather(val_words, val_bytes, "val")
        scores(qa_mx, 0)
        qb_g = deal(qb_raw, "qb_g")

        qb_mx = quantize_halves(qb_g, "qb")
        scores(qb_mx, 2)
        go_g = deal(go_raw, "go_g")
        ua = [tile([P, I], F32, f"ua{r}") for r in range(PACK)]
        vb = [tile([P, I], F32, f"vb{r}") for r in range(PACK)]
        for r in range(PACK):
            nc.scalar.activation(ua[r][:], pair(0, r), ACT.Sigmoid, bias=neg_th[:, r:r + 1], scale=1.0)
        for r in range(PACK):
            nc.scalar.activation(vb[r][:], pair(2, r), ACT.Sigmoid, bias=th_sb[:, r:r + 1], scale=-1.0)
        go_mx = quantize_halves(go_g, "go")

        vec_cols = tile([P, VEC_COLS], F32, "vec_cols")
        nc.tensor.transpose(banks[6][:, 0:P], vec_rows[:], ident[:])
        nc.scalar.copy(vec_cols[:], banks[6][:, 0:VEC_COLS])
        sized = [[tile([P, I], F32, f"sized{n}{h}") for h in range(2)] for n in range(2)]
        for n in range(2):
            rows = slice(n * I, (n + 1) * I)
            for h in range(2):
                cols = slice(h * P, (h + 1) * P)
                nc.tensor.matmul_mx(out=banks[4 + n][:, h * I:(h + 1) * I], lhsT=val_w[:, cols].bitcast(FP4X4), lhsT_scale=val_s[:, cols],
                                    rhs=go_mx[0][:, rows].bitcast(FP8X4), rhs_scale=go_mx[1][:, rows], start=True, stop=True)
        for n in range(2):
            for h in range(2):
                nc.scalar.activation(sized[n][h][:], banks[4 + n][:, h * I:(h + 1) * I], ACT.Copy,
                                     scale=vec_cols[:, SIZE_COL + h:SIZE_COL + h + 1])
            for r in (2 * n, 2 * n + 1):
                for h in range(2):
                    nc.tensor.transpose(pair(6, r)[:, h * P:(h + 1) * P], sized[n][h][:, (r % 2) * P:(r % 2 + 1) * P], ident[:])

        neg_m_pairs = [sb.tile([P, 2 * I], F32, name=f"neg_m{n}", tag=f"go_g{1 - n}", align_bytes=64) for n in range(2)]
        neg_m = [neg_m_pairs[r // 2][:, (r % 2) * I:(r % 2 + 1) * I] for r in range(PACK)]
        neg_m_sum = tile([P, PACK], F32, "neg_m_sum")
        for r in range(PACK):
            nc.vector.scalar_tensor_tensor(neg_m[r], ua[r][:], 1.0, vb[r][:], ALU.subtract, ALU.mult,
                                           accum_out=neg_m_sum[:, r:r + 1])
        z = tile([P, PACK], F32, "z")
        inv_z = tile([P, PACK], F32, "inv_z")
        factor = tile([P, PACK], F32, "factor")
        nc.vector.tensor_scalar(z[:], neg_m_sum[:], float(I), None, ALU.add)
        nc.vector.reciprocal(inv_z[:], z[:])
        nc.vector.scalar_tensor_tensor(factor[:], inv_z[:], -1.0, qs_sb[:], ALU.mult, ALU.mult)
        ua_scaled = tile([P, PACK * I], F32, "ua_scaled")
        for r in range(PACK):
            nc.scalar.activation(ua_scaled[:, r * I:(r + 1) * I], ua[r][:], ACT.Copy, scale=factor[:, r:r + 1])
        weighted = [tile([P, I], F32, f"weighted{n}") for n in range(2)]
        wsum = [tile([P, 1], F32, f"wsum{r}") for r in range(PACK)]
        mean = [tile([P, 1], F32, f"mean{r}") for r in range(PACK)]
        for r in range(PACK):
            nc.vector.scalar_tensor_tensor(weighted[r % 2][:], neg_m[r], 1.0, pair(6, r), ALU.add, ALU.mult,
                                           accum_out=wsum[r][:])
        for r in range(PACK):
            nc.vector.tensor_scalar(mean[r][:], wsum[r][:], inv_z[:, r:r + 1], None, ALU.mult)

        qr_g = [sb.tile([P, D * PACK // 2], BF16, name=f"qr_g{n}", tag=("sized11", "ua3")[n], align_bytes=64) for n in range(2)]
        qr_mx = [tile([P, D], U32, "qr_c"), tile([P, D], U8, "qr_s")]

        def quantize_qr(n):
            cols = slice(n * D // 2, (n + 1) * D // 2)
            nc.vector.quantize_mx(out=qr_mx[0][:, cols].bitcast(FP8X4), scales=qr_mx[1][:, cols], in_=qr_g[n][:])

        for n in range(2):
            nc.scalar.copy(qr_g[n][:].rearrange("p (c i r) -> p c r i", i=RUN, r=PACK),
                           qr_raw[:, :, n * 256:(n + 1) * 256].rearrange("p r (c i) -> p c r i", i=RUN))

        fade_wide = tile([P, BANK], F32, "fade_wide")
        for b in range(4):
            nc.tensor.transpose(banks[0][:, b * P:(b + 1) * P], vec_cols[:, FADE_COL + b:FADE_COL + b + 1].to_broadcast([P, P]), ident[:])
        nc.scalar.copy(fade_wide[:], banks[0][:])

        centred = tile([P, PACK * I], F32, "centred")
        for r in range(PACK):
            nc.vector.scalar_tensor_tensor(centred[:, r * I:(r + 1) * I], pair(6, r), mean[r][:], neg_m[r],
                                           ALU.subtract, ALU.mult)
        gs_g = [tile([P, P * PACK], BF16, f"gs_g{n}") for n in range(2)]
        gs_codes = tile([P, I], U32, "gs_codes")
        gs_scales = tile([P, I], U8, "gs_scales")

        def by_runs(t, pattern):
            return t[:].rearrange(pattern, i=RUN, r=PACK)

        def finish_gs(n):
            c = slice(n * 32, (n + 1) * 32)
            nc.vector.tensor_tensor(by_runs(gs_g[n], "p (c i r) -> p c r i"), by_runs(centred, "p (r c i) -> p c r i")[:, c],
                                    by_runs(ua_scaled, "p (r c i) -> p c r i")[:, c], ALU.mult)

        def quantize_gs(n):
            cols = slice(n * P, (n + 1) * P)
            nc.vector.quantize_mx(out=gs_codes[:, cols].bitcast(FP8X4), scales=gs_scales[:, cols],
                                  in_=gs_g[n][:])

        def key_gradient(k, first, last, tag):
            cols = slice(k * P, (k + 1) * P)
            nc.tensor.matmul_mx(out=banks[GK_BANK[k]][:, first:last], lhsT=qr_mx[0][:, cols].bitcast(FP8X4), lhsT_scale=qr_mx[1][:, cols],
                                rhs=gs_codes[:, first:last].bitcast(FP8X4), rhs_scale=gs_scales[:, first:last], start=True, stop=True)
            gk = sb.tile([P, last - first], F32, name=f"gk{k}_{first}", tag=tag, align_bytes=64)
            nc.scalar.copy(gk[:], banks[GK_BANK[k]][:, first:last])
            return gk

        def place(k, first, last, gk):
            nc.vector.tensor_copy(placed[k][:].indirect(places[:, first // 16:last // 16]), gk[:])

        finish_gs(0)
        quantize_qr(0)
        quantize_gs(0)
        finish_gs(1)
        early = [key_gradient(k, 0, P, f"gk_early{k}") for k in range(2)]
        quantize_gs(1)
        quantize_qr(1)
        for k in range(2):
            place(k, 0, P, early[k])
        for k in range(2):
            place(k, P, I, key_gradient(k, P, I, f"gk_late{k}"))
        place(2, 0, I, key_gradient(2, 0, I, "gk_late2"))

        results = [tile([P, U], F32, f"result{k}") for k in range(4)]

        def store(k, first, last):
            nc.sync.dma_start(out[k * P:(k + 1) * P, first:last], results[k][:, first:last])

        products = sb.tile([P, 3 * BANK], F32, name="products", tag="ua3", align_bytes=64)

        def gpsimd_fade(k):
            nc.gpsimd.tensor_tensor(products[:, k * BANK:(k + 1) * BANK], old_sb[0][:, k, :], fade_wide[:], ALU.mult)

        def gpsimd_add(k):
            nc.gpsimd.tensor_tensor(results[k][:, 0:BANK], products[:, k * BANK:(k + 1) * BANK], placed[k][:, 0:BANK], ALU.add)

        def vector_add(k, h, bank):
            cols = slice(h * BANK, (h + 1) * BANK)
            nc.vector.tensor_tensor(results[k][:, cols], bank[:], placed[k][:, cols], ALU.add)

        gpsimd_fade(0)
        gpsimd_fade(1)
        for k in range(2):
            gpsimd_add(k)
            store(k, 0, BANK)
        gpsimd_fade(2)
        gpsimd_add(2)

        faded = [tile([P, D], F32, f"faded{c}") for c in range(4)]
        for c in range(4):
            for k in range(4):
                nc.tensor.transpose(banks[FADE_BANK[c]][:, k * P:(k + 1) * P], old_sb[1][:, k, c * P:(c + 1) * P], ident[:])
            nc.scalar.activation(faded[c][:], banks[FADE_BANK[c]][:], ACT.Copy, scale=vec_cols[:, FADE_COL + 4 + c:FADE_COL + 5 + c])

        def turn_back(k, bank):
            for c in range(4):
                nc.tensor.transpose(bank[:, c * P:(c + 1) * P], faded[c][:, k * P:(k + 1) * P], ident[:])

        for k in range(4):
            turn_back(k, banks[k])
        last_gk = key_gradient(3, 0, I, "faded3")
        for k in range(3):
            vector_add(k, 1, banks[k])
            store(k, 0 if k == 2 else BANK, U)
        place(3, 0, I, last_gk)
        corner = [tile([P, P], F32, f"corner{c}") for c in range(4)]
        for c in range(4):
            nc.tensor.transpose(banks[5][:, c * P:(c + 1) * P], old_sb[0][:, 3, c * P:(c + 1) * P], ident[:])
        for c in range(4):
            nc.scalar.activation(corner[c][:], banks[5][:, c * P:(c + 1) * P], ACT.Copy,
                                 scale=vec_cols[:, FADE_COL + c:FADE_COL + c + 1])
        for c in range(4):
            nc.tensor.transpose(banks[6][:, c * P:(c + 1) * P], corner[c][:], ident[:])
        vector_add(3, 0, banks[6])
        store(3, 0, BANK)
        vector_add(3, 1, banks[3])
        store(3, BANK, U)
